import numpy as np
import ml_dtypes


def mxq(x, axis, fmt="e4m3"):
    dtype, down = {"e4m3": (ml_dtypes.float8_e4m3fn, 7), "e5m2": (ml_dtypes.float8_e5m2, 14)}[fmt]
    v = np.moveaxis(np.asarray(x, np.float32).astype(ml_dtypes.bfloat16).astype(np.float64), axis, -1)
    blocks = v.reshape(v.shape[:-1] + (-1, 32))
    amax = np.abs(blocks).max(-1, keepdims=True)
    byte = np.maximum(np.where(amax > 0, np.frexp(amax)[1] - 1 + 127, 0) - down, 1)
    scale = np.exp2(byte - 127.0)
    codes = (blocks / scale).astype(np.float32).astype(dtype).astype(np.float64)
    return np.moveaxis((codes * scale).reshape(v.shape), -1, axis)


WIDE = False


def mx_kscale(k):
    if not WIDE:
        return np.ones(k)
    levels = np.array([10, -10, 5, -5, 0])
    if k % 512:
        return np.exp2(np.random.permutation(np.resize(levels, k // 32))).repeat(32)
    a = np.empty((k // 512, 16))
    for p in range(k // 512):
        a[p, :8] = np.random.permutation(np.resize(levels, 8))
        for g in range(8):
            far = levels[np.abs(levels - a[p, g]) >= 10]
            a[p, g + 8] = far[np.random.randint(len(far))]
    return np.exp2(a.ravel()).repeat(32)


def f64(x):
    return np.asarray(x).astype(np.float64)


def striped8(idx):
    return np.asarray(idx).reshape(8, -1, 16).transpose(0, 2, 1).reshape(128, -1).astype(np.uint16)


def unstriped8(offs):
    return offs.reshape(8, 16, -1).transpose(0, 2, 1).reshape(8, -1).astype(np.int64)


def pick8(x, idx, run):
    r = np.arange(len(x))
    return x[r[:, None], idx[r % (8 * run) // run]]


E2M1 = np.array([0.0, 0.5, 1.0, 1.5, 2.0, 3.0, 4.0, 6.0, -0.0, -0.5, -1.0, -1.5, -2.0, -3.0, -4.0, -6.0])


def pack_weight(w, fmt):
    k, n = w.shape
    w = f64(np.asarray(w, np.float32).astype(ml_dtypes.bfloat16)).reshape(k // 32, 32, n)
    amax = np.abs(w).max(1)
    if fmt == "e4m3":
        byte = np.frexp(amax)[1] - 1 + 127 - 7
    else:
        mant, ex = np.frexp(amax / 6.0)
        byte = np.where(mant > 0.5, ex, ex - 1) + 127
    byte = np.clip(np.where(amax > 0, byte, 1), 1, 254)
    scaled = (w * np.exp2(127.0 - byte)[:, None, :]).reshape(k, n).astype(np.float32)
    by_word = np.ascontiguousarray(scaled.reshape(k // 512, 128, 4, n).transpose(0, 1, 3, 2))
    if fmt == "e4m3":
        words = by_word.astype(ml_dtypes.float8_e4m3fn).view(np.uint8)
    else:
        c = by_word.astype(ml_dtypes.float4_e2m1fn).view(np.uint8) & 0xF
        words = (c[..., 0::2] | (c[..., 1::2] << 4)).reshape(k // 512, 128, 2 * n)
    return np.ascontiguousarray(words), np.ascontiguousarray(byte.astype(np.uint8).reshape(k // 512, 16, n))


def unpack_weight(words, scales, fmt):
    g, _, n = scales.shape
    words = np.ascontiguousarray(words).reshape(g, 128, n, -1)
    if fmt == "e4m3":
        vals = words.view(ml_dtypes.float8_e4m3fn).astype(np.float64)
    else:
        nib = np.empty((g, 128, n, 4), np.uint8)
        nib[..., 0::2] = words & 0xF
        nib[..., 1::2] = words >> 4
        vals = E2M1[nib]
    vals = vals * np.repeat(np.exp2(scales.astype(np.float64) - 127.0), 8, axis=1)[..., None]
    return vals.transpose(0, 1, 3, 2).reshape(g * 512, n)


D, T, I, Q, G = 512, 1024, 512, 128, 64


def setup_inputs():
    n = np.random.standard_normal
    idx = np.stack([np.random.permutation(T)[:I] for _ in range(8)])
    idx2 = np.stack([np.random.permutation(T)[:I] for _ in range(8)])
    idx4 = np.stack([np.random.permutation(T)[:I] for _ in range(8)])
    fd = mx_kscale(D)
    keysp = pack_weight(n((D, T)) / fd[:, None], "e2m1")
    return {
        "query": (n((D, Q)) * 0.9 / np.sqrt(D) * fd[:, None]).astype(np.float32),
        "query2": (n((D, Q)) * 0.9 / np.sqrt(D) * fd[:, None]).astype(np.float32),
        "keys_words": keysp[0],
        "keys_scales": keysp[1],
        "lam": (np.random.uniform(0.5, 1.5, (Q, 1))).astype(np.float32),
        "bar": (np.random.uniform(0.6, 1.0, (Q, 1))).astype(np.float32),
        "reserve": (np.random.uniform(20.0, 80.0, (Q, 1))).astype(np.float32),
        "old": (np.random.uniform(0.0, 2.0, (Q, T))).astype(np.float32),
        "gainm": (np.random.uniform(0.5, 1.5, (Q, I))).astype(np.float32),
        "offs": striped8(idx),
        "offs2": striped8(idx2),
        "offs4": striped8(idx4),
    }


def reference(query, query2, keys_words, keys_scales, lam, bar, reserve, old, gainm, offs, offs2, offs4):
    idx = unstriped8(offs)
    idx2 = unstriped8(offs2)
    idx4 = unstriped8(offs4)
    keysu = unpack_weight(keys_words, keys_scales, "e2m1")
    queryq = mxq(f64(query), 0, "e4m3")
    a = queryq.T @ keysu
    query2q = mxq(f64(query2), 0, "e4m3")
    b = query2q.T @ keysu
    s = pick8(a, idx, 16) + pick8(a, idx2, 16) * np.tanh(pick8(b, idx, 16)) * f64(lam)
    p = np.exp(s)
    pm = p.reshape(Q, G, I // G).mean(axis=2)
    pr = np.repeat(pm, I // G, axis=1)
    r = np.maximum(p - pr * f64(bar), 0.0)
    w = r / (np.sum(r, axis=1, keepdims=True) + f64(reserve))
    ws = w * f64(gainm) * 256.0
    wf = np.zeros((Q, T))
    wf[np.arange(Q)[:, None], idx4[np.arange(Q) % 128 // 16]] = ws
    y = f64(old) + wf
    return y

@@ -1,0 +1,159 @@
+from contextlib import ExitStack
+
+import concourse.mybir as mybir
+
+D, T, SLOTS, Q, RUN = 512, 1024, 512, 128, 8
+FLOPS = 2 * 2 * D * Q * T
+
+F32 = mybir.dt.float32
+BF16 = mybir.dt.bfloat16
+I32 = mybir.dt.int32
+U32 = mybir.dt.uint32
+U16 = mybir.dt.uint16
+U8 = mybir.dt.uint8
+FP8X4 = mybir.dt.float8_e4m3fn_x4
+FP4X4 = mybir.dt.float4_e2m1fn_x4
+ALU = mybir.AluOpType
+ACT = mybir.ActivationFunctionType
+AXIS = mybir.AxisListType
+
+P = 128
+PACK = 4
+HALF = SLOTS // 2
+B_PIECES = ((0, 512), (512, 768), (768, 896), (896, 1024))
+A_PIECES = ((0, 256), (256, 512), (512, 768), (768, 1024))
+STORE_COLS = 256
+
+
+def tile_attend_turnedby_abovepage_moved_heads_kernel(
+    tc, query, query2, keys_words, keys_scales, lam, bar, reserve, old, gainm, offs, offs2, offs4, out
+):
+    nc = tc.nc
+    with ExitStack() as ctx:
+        sb = ctx.enter_context(tc.tile_pool(name="sb", bufs=1))
+        ps = ctx.enter_context(tc.psum_pool(name="ps", bufs=1))
+
+        key_scales = sb.tile([P, T], U8, name="key_scales", align_bytes=64)
+        key_words = sb.tile([P, 2 * T], U8, name="key_words", align_bytes=64)
+        raw_b = sb.tile([P, PACK, Q], F32, name="raw_b")
+        raw_a = sb.tile([P, PACK, Q], F32, name="raw_a")
+        idx = sb.tile([P, SLOTS // 16], U16, name="idx")
+        idx2 = sb.tile([P, SLOTS // 16], U16, name="idx2")
+        idx4 = sb.tile([P, SLOTS // 16], U16, name="idx4")
+        lam_col = sb.tile([P, 1], F32, name="lam_col")
+        bar_col = sb.tile([P, 1], F32, name="bar_col")
+        reserve_col = sb.tile([P, 1], F32, name="reserve_col")
+        gain = sb.tile([P, SLOTS], F32, name="gain")
+        counts = sb.tile([P, T], F32, name="counts")
+        placed = sb.tile([P, T], F32, name="placed")
+
+        nc.vector.memset(key_scales[:].bitcast(I32), 0)
+        nc.sync.dma_start(out=raw_b[:], in_=query2.rearrange("(p j) q -> p j q", j=PACK))
+        nc.sync.dma_start(out=raw_a[:], in_=query.rearrange("(p j) q -> p j q", j=PACK))
+        nc.sync.dma_start(out=key_words[:].bitcast(I32), in_=keys_words[0].bitcast(I32))
+        for quad in range(4):
+            nc.scalar.dma_start(
+                out=key_scales[32 * quad : 32 * quad + 4, :].bitcast(I32),
+                in_=keys_scales[0, 4 * quad : 4 * quad + 4, :].bitcast(I32),
+            )
+        nc.sync.dma_start(idx[:], offs)
+        nc.sync.dma_start(idx2[:], offs2)
+        nc.sync.dma_start(out=lam_col[:], in_=lam)
+        nc.sync.dma_start(out=bar_col[:], in_=bar)
+        nc.sync.dma_start(out=reserve_col[:], in_=reserve)
+        nc.sync.dma_start(out=gain[:], in_=gainm)
+        nc.sync.dma_start(idx4[:], offs4)
+        nc.sync.dma_start(out=counts[:], in_=old)
+        nc.vector.memset(placed[:], 0.0)
+
+        grouped_b = sb.tile([P, Q, PACK], BF16, name="grouped_b", align_bytes=64)
+        grouped_a = sb.tile([P, Q, PACK], BF16, name="grouped_a", align_bytes=64)
+        codes_b = sb.tile([P, Q], U32, name="codes_b", align_bytes=64)
+        codes_a = sb.tile([P, Q], U32, name="codes_a", align_bytes=64)
+        scales_b = sb.tile([P, Q], U8, name="scales_b", align_bytes=64)
+        scales_a = sb.tile([P, Q], U8, name="scales_a", align_bytes=64)
+
+        nc.vector.tensor_copy(out=grouped_b[:], in_=raw_b[:].rearrange("p j q -> p q j"))
+        nc.scalar.activation(out=grouped_a[:], in_=raw_a[:].rearrange("p j q -> p q j"), func=ACT.Copy)
+        for codes, scales, grouped in ((codes_b, scales_b, grouped_b), (codes_a, scales_a, grouped_a)):
+            nc.vector.quantize_mx(
+                out=codes[:].bitcast(FP8X4), scales=scales[:], in_=grouped[:].rearrange("p q j -> p (q j)")
+            )
+
+        a = sb.tile([P, T], F32, name="a")
+        b = sb.tile([P, T], F32, name="b")
+
+        def score(codes, scales, name, t0, t1):
+            bank = ps.tile([P, t1 - t0], F32, name=name)
+            nc.tensor.matmul_mx(
+                out=bank[:],
+                lhsT=codes[:].bitcast(FP8X4),
+                lhsT_scale=scales[:],
+                rhs=key_words[:, 2 * t0 : 2 * t1].bitcast(FP4X4),
+                rhs_scale=key_scales[:, t0:t1],
+                start=True,
+                stop=True,
+            )
+            return bank
+
+        for n, (t0, t1) in enumerate(B_PIECES):
+            bank = score(codes_b, scales_b, "bank_b%d" % n, t0, t1)
+            if n % 2 == 0:
+                nc.scalar.copy(out=b[:, t0:t1], in_=bank[:])
+            else:
+                nc.vector.tensor_copy(out=b[:, t0:t1], in_=bank[:])
+        for n, (t0, t1) in enumerate(A_PIECES):
+            bank = score(codes_a, scales_a, "bank_a%d" % n, t0, t1)
+            nc.vector.tensor_copy(out=a[:, t0:t1], in_=bank[:])
+
+        neg_bar = sb.tile([P, 1], F32, name="neg_bar")
+        nc.vector.tensor_scalar(neg_bar[:], bar_col[:], -1.0 / RUN, None, ALU.mult)
+
+        def half_tile(name):
+            return [sb.tile([P, HALF], F32, name="%s%d" % (name, h)) for h in range(2)]
+
+        b_at, turn, a_at, turned, s, p, diff = (half_tile(n) for n in ("b_at", "turn", "a_at", "turned", "s", "p", "diff"))
+        run_sum = [sb.tile([P, HALF // RUN], F32, name="run_sum%d" % h) for h in range(2)]
+        r = sb.tile([P, SLOTS], F32, name="r")
+        cols = [slice(h * HALF // 16, (h + 1) * HALF // 16) for h in range(2)]
+
+        for h in range(2):
+            nc.scalar.activation(out=b_at[h][:], in_=b[:].indirect(idx[:, cols[h]]), func=ACT.Copy)
+            nc.scalar.activation(out=turn[h][:], in_=b_at[h][:], func=ACT.Tanh)
+        for h in range(2):
+            nc.scalar.activation(out=a_at[h][:], in_=a[:].indirect(idx[:, cols[h]]), func=ACT.Copy)
+        for h in range(2):
+            nc.vector.tensor_tensor(turned[h][:], a[:].indirect(idx2[:, cols[h]]), turn[h][:], ALU.mult)
+        for h in range(2):
+            nc.vector.scalar_tensor_tensor(s[h][:], turned[h][:], lam_col[:], a_at[h][:], ALU.mult, ALU.add)
+            nc.scalar.activation(out=p[h][:], in_=s[h][:], func=ACT.Exp)
+        for h in range(2):
+            runs = p[h][:].rearrange("q (g e) -> q g e", e=RUN)
+            nc.vector.tensor_reduce(run_sum[h][:], runs, AXIS.X, ALU.add)
+            nc.vector.scalar_tensor_tensor(
+                diff[h][:].rearrange("q (g e) -> q g e", e=RUN),
+                run_sum[h][:].unsqueeze(2).to_broadcast([P, HALF // RUN, RUN]),
+                neg_bar[:],
+                runs,
+                ALU.mult,
+                ALU.add,
+            )
+
+        first_sum = sb.tile([P, 1], F32, name="first_sum")
+        start_sum = sb.tile([P, 1], F32, name="start_sum")
+        denom = sb.tile([P, 1], F32, name="denom")
+        inv = sb.tile([P, 1], F32, name="inv")
+        nc.scalar.activation(out=r[:, :HALF], in_=diff[0][:], func=ACT.Relu, accum_out=first_sum[:])
+        nc.vector.tensor_tensor(start_sum[:], first_sum[:], reserve_col[:], ALU.add)
+        nc.vector.tensor_scalar(r[:, HALF:], diff[1][:], 0.0, start_sum[:], ALU.max, ALU.add, accum_out=denom[:])
+        nc.vector.reciprocal(inv[:], denom[:])
+        w = sb.tile([P, SLOTS], F32, name="w")
+        nc.vector.tensor_scalar(w[:], r[:], inv[:], 256.0, ALU.mult, ALU.mult)
+        nc.vector.tensor_tensor(placed[:].indirect(idx4[:]), w[:], gain[:], ALU.mult)
+
+        for n, t0 in enumerate(range(0, T, STORE_COLS)):
+            piece = slice(t0, t0 + STORE_COLS)
+            result = sb.tile([P, STORE_COLS], F32, name="result%d" % n)
+            nc.vector.tensor_tensor(result[:], placed[:, piece], counts[:, piece], ALU.add)
+            queue = nc.sync if n % 2 == 0 else nc.scalar
+            queue.dma_start(out=out[:, piece], in_=result[:])

@@ -20,9 +20,10 @@ AXIS = mybir.AxisListType
 P = 128
 PACK = 4
 HALF = SLOTS // 2
+CAST_SPLIT = 72
 B_PIECES = ((0, 512), (512, 768), (768, 896), (896, 1024))
 A_PIECES = ((0, 256), (256, 512), (512, 768), (768, 1024))
-STORE_COLS = 256
+STORE_PIECES = ((0, 320), (320, 640), (640, 896), (896, 1024))
 
 
 def tile_attend_turnedby_abovepage_moved_heads_kernel(
@@ -49,8 +50,8 @@ def tile_attend_turnedby_abovepage_moved_heads_kernel(
 
         nc.vector.memset(key_scales[:].bitcast(I32), 0)
         nc.sync.dma_start(out=raw_b[:], in_=query2.rearrange("(p j) q -> p j q", j=PACK))
-        nc.sync.dma_start(out=raw_a[:], in_=query.rearrange("(p j) q -> p j q", j=PACK))
         nc.sync.dma_start(out=key_words[:].bitcast(I32), in_=keys_words[0].bitcast(I32))
+        nc.sync.dma_start(out=raw_a[:], in_=query.rearrange("(p j) q -> p j q", j=PACK))
         for quad in range(4):
             nc.scalar.dma_start(
                 out=key_scales[32 * quad : 32 * quad + 4, :].bitcast(I32),
@@ -73,7 +74,9 @@ def tile_attend_turnedby_abovepage_moved_heads_kernel(
         scales_b = sb.tile([P, Q], U8, name="scales_b", align_bytes=64)
         scales_a = sb.tile([P, Q], U8, name="scales_a", align_bytes=64)
 
-        nc.vector.tensor_copy(out=grouped_b[:], in_=raw_b[:].rearrange("p j q -> p q j"))
+        rows_b = raw_b[:].rearrange("p j q -> p q j")
+        nc.vector.tensor_copy(out=grouped_b[:, :CAST_SPLIT, :], in_=rows_b[:, :CAST_SPLIT, :])
+        nc.scalar.activation(out=grouped_b[:, CAST_SPLIT:, :], in_=rows_b[:, CAST_SPLIT:, :], func=ACT.Copy)
         nc.scalar.activation(out=grouped_a[:], in_=raw_a[:].rearrange("p j q -> p q j"), func=ACT.Copy)
         for codes, scales, grouped in ((codes_b, scales_b, grouped_b), (codes_a, scales_a, grouped_a)):
             nc.vector.quantize_mx(
@@ -99,12 +102,12 @@ def tile_attend_turnedby_abovepage_moved_heads_kernel(
         for n, (t0, t1) in enumerate(B_PIECES):
             bank = score(codes_b, scales_b, "bank_b%d" % n, t0, t1)
             if n % 2 == 0:
-                nc.scalar.copy(out=b[:, t0:t1], in_=bank[:])
+                nc.scalar.activation(out=b[:, t0:t1], in_=bank[:], func=ACT.Copy)
             else:
                 nc.vector.tensor_copy(out=b[:, t0:t1], in_=bank[:])
-        for n, (t0, t1) in enumerate(A_PIECES):
-            bank = score(codes_a, scales_a, "bank_a%d" % n, t0, t1)
-            nc.vector.tensor_copy(out=a[:, t0:t1], in_=bank[:])
+        banks_a = [score(codes_a, scales_a, name, t0, t1) for name, (t0, t1) in zip(("bank_a0", "bank_a1", "bank_b2", "bank_b0"), A_PIECES)]
+        a_cols = [slice(t0, t1) for t0, t1 in A_PIECES]
+        nc.vector.tensor_copy(out=a[:, a_cols[0]], in_=banks_a[0][:])
 
         neg_bar = sb.tile([P, 1], F32, name="neg_bar")
         nc.vector.tensor_scalar(neg_bar[:], bar_col[:], -1.0 / RUN, None, ALU.mult)
@@ -112,26 +115,39 @@ def tile_attend_turnedby_abovepage_moved_heads_kernel(
         def half_tile(name):
             return [sb.tile([P, HALF], F32, name="%s%d" % (name, h)) for h in range(2)]
 
-        b_at, turn, a_at, turned, s, p, diff = (half_tile(n) for n in ("b_at", "turn", "a_at", "turned", "s", "p", "diff"))
+        turn, turned, p = (half_tile(n) for n in ("turn", "turned", "p"))
+        s = sb.tile([P, SLOTS], F32, name="s", tag="s_then_diff")
+        halves = [slice(h * HALF, (h + 1) * HALF) for h in range(2)]
+        b_picked = sb.tile([P, SLOTS], F32, name="b_picked", tag="picked")
+        b_at = [b_picked[:, :HALF], b_picked[:, HALF:]]
         run_sum = [sb.tile([P, HALF // RUN], F32, name="run_sum%d" % h) for h in range(2)]
         r = sb.tile([P, SLOTS], F32, name="r")
         cols = [slice(h * HALF // 16, (h + 1) * HALF // 16) for h in range(2)]
 
+        nc.vector.tensor_copy(out=b_at[0], in_=b[:].indirect(idx[:, cols[0]]))
+        nc.scalar.activation(out=b_at[1], in_=b[:].indirect(idx[:, cols[1]]), func=ACT.Copy)
+        nc.scalar.activation(out=a[:, a_cols[1]], in_=banks_a[1][:], func=ACT.Copy)
+        for n in (2, 3):
+            nc.vector.tensor_copy(out=a[:, a_cols[n]], in_=banks_a[n][:])
         for h in range(2):
-            nc.scalar.activation(out=b_at[h][:], in_=b[:].indirect(idx[:, cols[h]]), func=ACT.Copy)
-            nc.scalar.activation(out=turn[h][:], in_=b_at[h][:], func=ACT.Tanh)
+            nc.scalar.activation(out=turn[h][:], in_=b_at[h], func=ACT.Tanh)
+        a_picked = sb.tile([P, SLOTS], F32, name="a_picked", tag="picked")
+        a_at = [a_picked[:, :HALF], a_picked[:, HALF:]]
         for h in range(2):
-            nc.scalar.activation(out=a_at[h][:], in_=a[:].indirect(idx[:, cols[h]]), func=ACT.Copy)
+            nc.scalar.activation(out=a_at[h], in_=a[:].indirect(idx[:, cols[h]]), func=ACT.Copy)
         for h in range(2):
             nc.vector.tensor_tensor(turned[h][:], a[:].indirect(idx2[:, cols[h]]), turn[h][:], ALU.mult)
         for h in range(2):
-            nc.vector.scalar_tensor_tensor(s[h][:], turned[h][:], lam_col[:], a_at[h][:], ALU.mult, ALU.add)
-            nc.scalar.activation(out=p[h][:], in_=s[h][:], func=ACT.Exp)
+            nc.vector.scalar_tensor_tensor(s[:, halves[h]], turned[h][:], lam_col[:], a_at[h], ALU.mult, ALU.add)
+            nc.scalar.activation(out=p[h][:], in_=s[:, halves[h]], func=ACT.Exp)
         for h in range(2):
             runs = p[h][:].rearrange("q (g e) -> q g e", e=RUN)
             nc.vector.tensor_reduce(run_sum[h][:], runs, AXIS.X, ALU.add)
+        diff = sb.tile([P, SLOTS], F32, name="diff", tag="s_then_diff")
+        for h in range(2):
+            runs = p[h][:].rearrange("q (g e) -> q g e", e=RUN)
             nc.vector.scalar_tensor_tensor(
-                diff[h][:].rearrange("q (g e) -> q g e", e=RUN),
+                diff[:, h * HALF : (h + 1) * HALF].rearrange("q (g e) -> q g e", e=RUN),
                 run_sum[h][:].unsqueeze(2).to_broadcast([P, HALF // RUN, RUN]),
                 neg_bar[:],
                 runs,
@@ -139,21 +155,22 @@ def tile_attend_turnedby_abovepage_moved_heads_kernel(
                 ALU.add,
             )
 
-        first_sum = sb.tile([P, 1], F32, name="first_sum")
-        start_sum = sb.tile([P, 1], F32, name="start_sum")
         denom = sb.tile([P, 1], F32, name="denom")
         inv = sb.tile([P, 1], F32, name="inv")
-        nc.scalar.activation(out=r[:, :HALF], in_=diff[0][:], func=ACT.Relu, accum_out=first_sum[:])
-        nc.vector.tensor_tensor(start_sum[:], first_sum[:], reserve_col[:], ALU.add)
-        nc.vector.tensor_scalar(r[:, HALF:], diff[1][:], 0.0, start_sum[:], ALU.max, ALU.add, accum_out=denom[:])
+        half_sum = sb.tile([P, 2], F32, name="half_sum")
+        for h in range(2):
+            nc.scalar.activation(
+                out=r[:, halves[h]], in_=diff[:, halves[h]], func=ACT.Relu, accum_out=half_sum[:, h : h + 1]
+            )
+        nc.vector.tensor_scalar(denom[:], half_sum[:, 1:2], half_sum[:, 0:1], reserve_col[:], ALU.add, ALU.add)
         nc.vector.reciprocal(inv[:], denom[:])
         w = sb.tile([P, SLOTS], F32, name="w")
         nc.vector.tensor_scalar(w[:], r[:], inv[:], 256.0, ALU.mult, ALU.mult)
         nc.vector.tensor_tensor(placed[:].indirect(idx4[:]), w[:], gain[:], ALU.mult)
 
-        for n, t0 in enumerate(range(0, T, STORE_COLS)):
-            piece = slice(t0, t0 + STORE_COLS)
-            result = sb.tile([P, STORE_COLS], F32, name="result%d" % n)
+        for n, (t0, t1) in enumerate(STORE_PIECES):
+            piece = slice(t0, t1)
+            result = sb.tile([P, t1 - t0], F32, name="result%d" % n)
             nc.vector.tensor_tensor(result[:], placed[:, piece], counts[:, piece], ALU.add)
             queue = nc.sync if n % 2 == 0 else nc.scalar
             queue.dma_start(out=out[:, piece], in_=result[:])

@@ -20,7 +20,7 @@ AXIS = mybir.AxisListType
 P = 128
 PACK = 4
 HALF = SLOTS // 2
-CAST_SPLIT = 72
+CAST_SPLIT = 80
 B_PIECES = ((0, 512), (512, 768), (768, 896), (896, 1024))
 A_PIECES = ((0, 256), (256, 512), (512, 768), (768, 1024))
 STORE_PIECES = ((0, 320), (320, 640), (640, 896), (896, 1024))
@@ -35,7 +35,7 @@ def tile_attend_turnedby_abovepage_moved_heads_kernel(
         ps = ctx.enter_context(tc.psum_pool(name="ps", bufs=1))
 
         key_scales = sb.tile([P, T], U8, name="key_scales", align_bytes=64)
-        key_words = sb.tile([P, 2 * T], U8, name="key_words", align_bytes=64)
+        key_words = [sb.tile([P, T], U8, name="key_words%d" % n, align_bytes=64) for n in range(2)]
         raw_b = sb.tile([P, PACK, Q], F32, name="raw_b")
         raw_a = sb.tile([P, PACK, Q], F32, name="raw_a")
         idx = sb.tile([P, SLOTS // 16], U16, name="idx")
@@ -50,8 +50,9 @@ def tile_attend_turnedby_abovepage_moved_heads_kernel(
 
         nc.vector.memset(key_scales[:].bitcast(I32), 0)
         nc.sync.dma_start(out=raw_b[:], in_=query2.rearrange("(p j) q -> p j q", j=PACK))
-        nc.sync.dma_start(out=key_words[:].bitcast(I32), in_=keys_words[0].bitcast(I32))
+        nc.sync.dma_start(out=key_words[0][:].bitcast(I32), in_=keys_words[0, :, :T].bitcast(I32))
         nc.sync.dma_start(out=raw_a[:], in_=query.rearrange("(p j) q -> p j q", j=PACK))
+        nc.sync.dma_start(out=key_words[1][:].bitcast(I32), in_=keys_words[0, :, T:].bitcast(I32))
         for quad in range(4):
             nc.scalar.dma_start(
                 out=key_scales[32 * quad : 32 * quad + 4, :].bitcast(I32),
@@ -67,18 +68,16 @@ def tile_attend_turnedby_abovepage_moved_heads_kernel(
         nc.sync.dma_start(out=counts[:], in_=old)
         nc.vector.memset(placed[:], 0.0)
 
-        grouped_b = sb.tile([P, Q, PACK], BF16, name="grouped_b", align_bytes=64)
-        grouped_a = sb.tile([P, Q, PACK], BF16, name="grouped_a", align_bytes=64)
         codes_b = sb.tile([P, Q], U32, name="codes_b", align_bytes=64)
         codes_a = sb.tile([P, Q], U32, name="codes_a", align_bytes=64)
         scales_b = sb.tile([P, Q], U8, name="scales_b", align_bytes=64)
         scales_a = sb.tile([P, Q], U8, name="scales_a", align_bytes=64)
 
-        rows_b = raw_b[:].rearrange("p j q -> p q j")
-        nc.vector.tensor_copy(out=grouped_b[:, :CAST_SPLIT, :], in_=rows_b[:, :CAST_SPLIT, :])
-        nc.scalar.activation(out=grouped_b[:, CAST_SPLIT:, :], in_=rows_b[:, CAST_SPLIT:, :], func=ACT.Copy)
-        nc.scalar.activation(out=grouped_a[:], in_=raw_a[:].rearrange("p j q -> p q j"), func=ACT.Copy)
-        for codes, scales, grouped in ((codes_b, scales_b, grouped_b), (codes_a, scales_a, grouped_a)):
+        for raw, codes, scales in ((raw_b, codes_b, scales_b), (raw_a, codes_a, scales_a)):
+            grouped = sb.tile([P, Q, PACK], BF16, name="grouped", align_bytes=64)
+            rows = raw[:].rearrange("p j q -> p q j")
+            nc.vector.tensor_copy(out=grouped[:, :CAST_SPLIT, :], in_=rows[:, :CAST_SPLIT, :])
+            nc.scalar.activation(out=grouped[:, CAST_SPLIT:, :], in_=rows[:, CAST_SPLIT:, :], func=ACT.Copy)
             nc.vector.quantize_mx(
                 out=codes[:].bitcast(FP8X4), scales=scales[:], in_=grouped[:].rearrange("p q j -> p (q j)")
             )
@@ -92,7 +91,7 @@ def tile_attend_turnedby_abovepage_moved_heads_kernel(
                 out=bank[:],
                 lhsT=codes[:].bitcast(FP8X4),
                 lhsT_scale=scales[:],
-                rhs=key_words[:, 2 * t0 : 2 * t1].bitcast(FP4X4),
+                rhs=key_words[t0 // 512][:, 2 * (t0 % 512) : 2 * (t0 % 512 + t1 - t0)].bitcast(FP4X4),
                 rhs_scale=key_scales[:, t0:t1],
                 start=True,
                 stop=True,
@@ -107,7 +106,8 @@ def tile_attend_turnedby_abovepage_moved_heads_kernel(
                 nc.vector.tensor_copy(out=b[:, t0:t1], in_=bank[:])
         banks_a = [score(codes_a, scales_a, name, t0, t1) for name, (t0, t1) in zip(("bank_a0", "bank_a1", "bank_b2", "bank_b0"), A_PIECES)]
         a_cols = [slice(t0, t1) for t0, t1 in A_PIECES]
-        nc.vector.tensor_copy(out=a[:, a_cols[0]], in_=banks_a[0][:])
+        for n in (0, 1):
+            nc.vector.tensor_copy(out=a[:, a_cols[n]], in_=banks_a[n][:])
 
         neg_bar = sb.tile([P, 1], F32, name="neg_bar")
         nc.vector.tensor_scalar(neg_bar[:], bar_col[:], -1.0 / RUN, None, ALU.mult)
@@ -118,20 +118,19 @@ def tile_attend_turnedby_abovepage_moved_heads_kernel(
         turn, turned, p = (half_tile(n) for n in ("turn", "turned", "p"))
         s = sb.tile([P, SLOTS], F32, name="s", tag="s_then_diff")
         halves = [slice(h * HALF, (h + 1) * HALF) for h in range(2)]
-        b_picked = sb.tile([P, SLOTS], F32, name="b_picked", tag="picked")
+        b_picked = sb.tile([P, SLOTS], F32, name="b_picked")
         b_at = [b_picked[:, :HALF], b_picked[:, HALF:]]
         run_sum = [sb.tile([P, HALF // RUN], F32, name="run_sum%d" % h) for h in range(2)]
         r = sb.tile([P, SLOTS], F32, name="r")
         cols = [slice(h * HALF // 16, (h + 1) * HALF // 16) for h in range(2)]
 
-        nc.vector.tensor_copy(out=b_at[0], in_=b[:].indirect(idx[:, cols[0]]))
-        nc.scalar.activation(out=b_at[1], in_=b[:].indirect(idx[:, cols[1]]), func=ACT.Copy)
-        nc.scalar.activation(out=a[:, a_cols[1]], in_=banks_a[1][:], func=ACT.Copy)
-        for n in (2, 3):
-            nc.vector.tensor_copy(out=a[:, a_cols[n]], in_=banks_a[n][:])
+        nc.scalar.activation(out=b_at[0], in_=b[:].indirect(idx[:, cols[0]]), func=ACT.Copy)
+        nc.vector.tensor_copy(out=b_at[1], in_=b[:].indirect(idx[:, cols[1]]))
+        nc.scalar.activation(out=a[:, a_cols[2]], in_=banks_a[2][:], func=ACT.Copy)
+        nc.vector.tensor_copy(out=a[:, a_cols[3]], in_=banks_a[3][:])
         for h in range(2):
             nc.scalar.activation(out=turn[h][:], in_=b_at[h], func=ACT.Tanh)
-        a_picked = sb.tile([P, SLOTS], F32, name="a_picked", tag="picked")
+        a_picked = sb.tile([P, SLOTS], F32, name="a_picked")
         a_at = [a_picked[:, :HALF], a_picked[:, HALF:]]
         for h in range(2):
             nc.scalar.activation(out=a_at[h], in_=a[:].indirect(idx[:, cols[h]]), func=ACT.Copy)

@@ -19,10 +19,16 @@ AXIS = mybir.AxisListType
 
 P = 128
 PACK = 4
+QUADRANT = 32
+SCALE_ROWS = 4
+LIST_ROWS = 16
+WORD_BYTES = 2
+KEY_TOKENS = T // 2
 HALF = SLOTS // 2
 CAST_SPLIT = 80
 B_PIECES = ((0, 512), (512, 768), (768, 896), (896, 1024))
 A_PIECES = ((0, 256), (256, 512), (512, 768), (768, 1024))
+A_BANKS = ("bank_a0", "bank_a1", "bank_b2", "bank_b0")
 STORE_PIECES = ((0, 320), (320, 640), (640, 896), (896, 1024))
 
 
@@ -34,13 +40,14 @@ def tile_attend_turnedby_abovepage_moved_heads_kernel(
         sb = ctx.enter_context(tc.tile_pool(name="sb", bufs=1))
         ps = ctx.enter_context(tc.psum_pool(name="ps", bufs=1))
 
+        key_bytes = WORD_BYTES * KEY_TOKENS
         key_scales = sb.tile([P, T], U8, name="key_scales", align_bytes=64)
-        key_words = [sb.tile([P, T], U8, name="key_words%d" % n, align_bytes=64) for n in range(2)]
+        key_words = [sb.tile([P, key_bytes], U8, name="key_words%d" % n, align_bytes=64) for n in range(2)]
         raw_b = sb.tile([P, PACK, Q], F32, name="raw_b")
         raw_a = sb.tile([P, PACK, Q], F32, name="raw_a")
-        idx = sb.tile([P, SLOTS // 16], U16, name="idx")
-        idx2 = sb.tile([P, SLOTS // 16], U16, name="idx2")
-        idx4 = sb.tile([P, SLOTS // 16], U16, name="idx4")
+        idx = sb.tile([P, SLOTS // LIST_ROWS], U16, name="idx")
+        idx2 = sb.tile([P, SLOTS // LIST_ROWS], U16, name="idx2")
+        idx4 = sb.tile([P, SLOTS // LIST_ROWS], U16, name="idx4")
         lam_col = sb.tile([P, 1], F32, name="lam_col")
         bar_col = sb.tile([P, 1], F32, name="bar_col")
         reserve_col = sb.tile([P, 1], F32, name="reserve_col")
@@ -50,14 +57,15 @@ def tile_attend_turnedby_abovepage_moved_heads_kernel(
 
         nc.vector.memset(key_scales[:].bitcast(I32), 0)
         nc.sync.dma_start(out=raw_b[:], in_=query2.rearrange("(p j) q -> p j q", j=PACK))
-        nc.sync.dma_start(out=key_words[0][:].bitcast(I32), in_=keys_words[0, :, :T].bitcast(I32))
-        nc.sync.dma_start(out=raw_a[:], in_=query.rearrange("(p j) q -> p j q", j=PACK))
-        nc.sync.dma_start(out=key_words[1][:].bitcast(I32), in_=keys_words[0, :, T:].bitcast(I32))
-        for quad in range(4):
-            nc.scalar.dma_start(
-                out=key_scales[32 * quad : 32 * quad + 4, :].bitcast(I32),
-                in_=keys_scales[0, 4 * quad : 4 * quad + 4, :].bitcast(I32),
+        nc.sync.dma_start(out=key_words[0][:].bitcast(I32), in_=keys_words[0, :, :key_bytes].bitcast(I32))
+        for quad in range(P // QUADRANT):
+            queue = nc.sync if quad % 2 == 0 else nc.scalar
+            queue.dma_start(
+                out=key_scales[QUADRANT * quad : QUADRANT * quad + SCALE_ROWS, :].bitcast(I32),
+                in_=keys_scales[0, SCALE_ROWS * quad : SCALE_ROWS * (quad + 1), :].bitcast(I32),
             )
+        nc.sync.dma_start(out=raw_a[:], in_=query.rearrange("(p j) q -> p j q", j=PACK))
+        nc.sync.dma_start(out=key_words[1][:].bitcast(I32), in_=keys_words[0, :, key_bytes:].bitcast(I32))
         nc.sync.dma_start(idx[:], offs)
         nc.sync.dma_start(idx2[:], offs2)
         nc.sync.dma_start(out=lam_col[:], in_=lam)
@@ -85,13 +93,14 @@ def tile_attend_turnedby_abovepage_moved_heads_kernel(
         a = sb.tile([P, T], F32, name="a")
         b = sb.tile([P, T], F32, name="b")
 
-        def score(codes, scales, name, t0, t1):
-            bank = ps.tile([P, t1 - t0], F32, name=name)
+        def score(codes, scales, bank_name, t0, t1):
+            bank = ps.tile([P, t1 - t0], F32, name=bank_name)
+            load, first = divmod(t0, KEY_TOKENS)
             nc.tensor.matmul_mx(
                 out=bank[:],
                 lhsT=codes[:].bitcast(FP8X4),
                 lhsT_scale=scales[:],
-                rhs=key_words[t0 // 512][:, 2 * (t0 % 512) : 2 * (t0 % 512 + t1 - t0)].bitcast(FP4X4),
+                rhs=key_words[load][:, WORD_BYTES * first : WORD_BYTES * (first + t1 - t0)].bitcast(FP4X4),
                 rhs_scale=key_scales[:, t0:t1],
                 start=True,
                 stop=True,
@@ -104,52 +113,53 @@ def tile_attend_turnedby_abovepage_moved_heads_kernel(
                 nc.scalar.activation(out=b[:, t0:t1], in_=bank[:], func=ACT.Copy)
             else:
                 nc.vector.tensor_copy(out=b[:, t0:t1], in_=bank[:])
-        banks_a = [score(codes_a, scales_a, name, t0, t1) for name, (t0, t1) in zip(("bank_a0", "bank_a1", "bank_b2", "bank_b0"), A_PIECES)]
+        banks_a = [score(codes_a, scales_a, name, t0, t1) for name, (t0, t1) in zip(A_BANKS, A_PIECES)]
         a_cols = [slice(t0, t1) for t0, t1 in A_PIECES]
-        for n in (0, 1):
+        for n in range(2):
             nc.vector.tensor_copy(out=a[:, a_cols[n]], in_=banks_a[n][:])
 
         neg_bar = sb.tile([P, 1], F32, name="neg_bar")
-        nc.vector.tensor_scalar(neg_bar[:], bar_col[:], -1.0 / RUN, None, ALU.mult)
+        nc.gpsimd.tensor_scalar(neg_bar[:], bar_col[:], -1.0 / RUN, 0.0, ALU.mult, ALU.add)
 
-        def half_tile(name):
+        def half_tiles(name):
             return [sb.tile([P, HALF], F32, name="%s%d" % (name, h)) for h in range(2)]
 
-        turn, turned, p = (half_tile(n) for n in ("turn", "turned", "p"))
+        tanh_b, a2_tanh_b, exp_s = (half_tiles(name) for name in ("tanh_b", "a2_tanh_b", "exp_s"))
         s = sb.tile([P, SLOTS], F32, name="s", tag="s_then_diff")
         halves = [slice(h * HALF, (h + 1) * HALF) for h in range(2)]
         b_picked = sb.tile([P, SLOTS], F32, name="b_picked")
-        b_at = [b_picked[:, :HALF], b_picked[:, HALF:]]
         run_sum = [sb.tile([P, HALF // RUN], F32, name="run_sum%d" % h) for h in range(2)]
         r = sb.tile([P, SLOTS], F32, name="r")
-        cols = [slice(h * HALF // 16, (h + 1) * HALF // 16) for h in range(2)]
+        list_cols = [slice(h * HALF // LIST_ROWS, (h + 1) * HALF // LIST_ROWS) for h in range(2)]
 
-        nc.scalar.activation(out=b_at[0], in_=b[:].indirect(idx[:, cols[0]]), func=ACT.Copy)
-        nc.vector.tensor_copy(out=b_at[1], in_=b[:].indirect(idx[:, cols[1]]))
+        nc.scalar.activation(out=b_picked[:, halves[0]], in_=b[:].indirect(idx[:, list_cols[0]]), func=ACT.Copy)
+        nc.vector.tensor_copy(out=b_picked[:, halves[1]], in_=b[:].indirect(idx[:, list_cols[1]]))
         nc.scalar.activation(out=a[:, a_cols[2]], in_=banks_a[2][:], func=ACT.Copy)
         nc.vector.tensor_copy(out=a[:, a_cols[3]], in_=banks_a[3][:])
         for h in range(2):
-            nc.scalar.activation(out=turn[h][:], in_=b_at[h], func=ACT.Tanh)
+            nc.scalar.activation(out=tanh_b[h][:], in_=b_picked[:, halves[h]], func=ACT.Tanh)
+
         a_picked = sb.tile([P, SLOTS], F32, name="a_picked")
-        a_at = [a_picked[:, :HALF], a_picked[:, HALF:]]
         for h in range(2):
-            nc.scalar.activation(out=a_at[h], in_=a[:].indirect(idx[:, cols[h]]), func=ACT.Copy)
+            nc.scalar.activation(out=a_picked[:, halves[h]], in_=a[:].indirect(idx[:, list_cols[h]]), func=ACT.Copy)
         for h in range(2):
-            nc.vector.tensor_tensor(turned[h][:], a[:].indirect(idx2[:, cols[h]]), turn[h][:], ALU.mult)
+            nc.vector.tensor_tensor(a2_tanh_b[h][:], a[:].indirect(idx2[:, list_cols[h]]), tanh_b[h][:], ALU.mult)
         for h in range(2):
-            nc.vector.scalar_tensor_tensor(s[:, halves[h]], turned[h][:], lam_col[:], a_at[h], ALU.mult, ALU.add)
-            nc.scalar.activation(out=p[h][:], in_=s[:, halves[h]], func=ACT.Exp)
+            nc.vector.scalar_tensor_tensor(
+                s[:, halves[h]], a2_tanh_b[h][:], lam_col[:], a_picked[:, halves[h]], ALU.mult, ALU.add
+            )
+            nc.scalar.activation(out=exp_s[h][:], in_=s[:, halves[h]], func=ACT.Exp)
+
+        runs = [exp_s[h][:].rearrange("q (g e) -> q g e", e=RUN) for h in range(2)]
         for h in range(2):
-            runs = p[h][:].rearrange("q (g e) -> q g e", e=RUN)
-            nc.vector.tensor_reduce(run_sum[h][:], runs, AXIS.X, ALU.add)
+            nc.vector.tensor_reduce(run_sum[h][:], runs[h], AXIS.X, ALU.add)
         diff = sb.tile([P, SLOTS], F32, name="diff", tag="s_then_diff")
         for h in range(2):
-            runs = p[h][:].rearrange("q (g e) -> q g e", e=RUN)
             nc.vector.scalar_tensor_tensor(
-                diff[:, h * HALF : (h + 1) * HALF].rearrange("q (g e) -> q g e", e=RUN),
+                diff[:, halves[h]].rearrange("q (g e) -> q g e", e=RUN),
                 run_sum[h][:].unsqueeze(2).to_broadcast([P, HALF // RUN, RUN]),
                 neg_bar[:],
-                runs,
+                runs[h],
                 ALU.mult,
                 ALU.add,
             )
@@ -163,9 +173,10 @@ def tile_attend_turnedby_abovepage_moved_heads_kernel(
             )
         nc.vector.tensor_scalar(denom[:], half_sum[:, 1:2], half_sum[:, 0:1], reserve_col[:], ALU.add, ALU.add)
         nc.vector.reciprocal(inv[:], denom[:])
-        w = sb.tile([P, SLOTS], F32, name="w")
-        nc.vector.tensor_scalar(w[:], r[:], inv[:], 256.0, ALU.mult, ALU.mult)
-        nc.vector.tensor_tensor(placed[:].indirect(idx4[:]), w[:], gain[:], ALU.mult)
+
+        w256 = sb.tile([P, SLOTS], F32, name="w256")
+        nc.vector.tensor_scalar(w256[:], r[:], inv[:], 256.0, ALU.mult, ALU.mult)
+        nc.vector.tensor_tensor(placed[:].indirect(idx4[:]), w256[:], gain[:], ALU.mult)
 
         for n, (t0, t1) in enumerate(STORE_PIECES):
             piece = slice(t0, t1)

from contextlib import ExitStack

import concourse.mybir as mybir

D, T, SLOTS, Q, RUN = 512, 1024, 512, 128, 8
FLOPS = 2 * 2 * D * Q * T

F32 = mybir.dt.float32
BF16 = mybir.dt.bfloat16
I32 = mybir.dt.int32
U32 = mybir.dt.uint32
U16 = mybir.dt.uint16
U8 = mybir.dt.uint8
FP8X4 = mybir.dt.float8_e4m3fn_x4
FP4X4 = mybir.dt.float4_e2m1fn_x4
ALU = mybir.AluOpType
ACT = mybir.ActivationFunctionType
AXIS = mybir.AxisListType

P = 128
PACK = 4
QUADRANT = 32
SCALE_ROWS = 4
LIST_ROWS = 16
WORD_BYTES = 2
KEY_TOKENS = T // 2
HALF = SLOTS // 2
CAST_SPLIT = 80
B_PIECES = ((0, 512), (512, 768), (768, 896), (896, 1024))
A_PIECES = ((0, 256), (256, 512), (512, 768), (768, 1024))
A_BANKS = ("bank_a0", "bank_a1", "bank_b2", "bank_b0")
STORE_PIECES = ((0, 320), (320, 640), (640, 896), (896, 1024))


def tile_attend_turnedby_abovepage_moved_heads_kernel(
    tc, query, query2, keys_words, keys_scales, lam, bar, reserve, old, gainm, offs, offs2, offs4, out
):
    nc = tc.nc
    with ExitStack() as ctx:
        sb = ctx.enter_context(tc.tile_pool(name="sb", bufs=1))
        ps = ctx.enter_context(tc.psum_pool(name="ps", bufs=1))

        key_bytes = WORD_BYTES * KEY_TOKENS
        key_scales = sb.tile([P, T], U8, name="key_scales", align_bytes=64)
        key_words = [sb.tile([P, key_bytes], U8, name="key_words%d" % n, align_bytes=64) for n in range(2)]
        raw_b = sb.tile([P, PACK, Q], F32, name="raw_b")
        raw_a = sb.tile([P, PACK, Q], F32, name="raw_a")
        idx = sb.tile([P, SLOTS // LIST_ROWS], U16, name="idx")
        idx2 = sb.tile([P, SLOTS // LIST_ROWS], U16, name="idx2")
        idx4 = sb.tile([P, SLOTS // LIST_ROWS], U16, name="idx4")
        lam_col = sb.tile([P, 1], F32, name="lam_col")
        bar_col = sb.tile([P, 1], F32, name="bar_col")
        reserve_col = sb.tile([P, 1], F32, name="reserve_col")
        gain = sb.tile([P, SLOTS], F32, name="gain")
        counts = sb.tile([P, T], F32, name="counts")
        placed = sb.tile([P, T], F32, name="placed")

        nc.vector.memset(key_scales[:].bitcast(I32), 0)
        nc.sync.dma_start(out=raw_b[:], in_=query2.rearrange("(p j) q -> p j q", j=PACK))
        nc.sync.dma_start(out=key_words[0][:].bitcast(I32), in_=keys_words[0, :, :key_bytes].bitcast(I32))
        for quad in range(P // QUADRANT):
            queue = nc.sync if quad % 2 == 0 else nc.scalar
            queue.dma_start(
                out=key_scales[QUADRANT * quad : QUADRANT * quad + SCALE_ROWS, :].bitcast(I32),
                in_=keys_scales[0, SCALE_ROWS * quad : SCALE_ROWS * (quad + 1), :].bitcast(I32),
            )
        nc.sync.dma_start(out=raw_a[:], in_=query.rearrange("(p j) q -> p j q", j=PACK))
        nc.sync.dma_start(out=key_words[1][:].bitcast(I32), in_=keys_words[0, :, key_bytes:].bitcast(I32))
        nc.sync.dma_start(idx[:], offs)
        nc.sync.dma_start(idx2[:], offs2)
        nc.sync.dma_start(out=lam_col[:], in_=lam)
        nc.sync.dma_start(out=bar_col[:], in_=bar)
        nc.sync.dma_start(out=reserve_col[:], in_=reserve)
        nc.sync.dma_start(out=gain[:], in_=gainm)
        nc.sync.dma_start(idx4[:], offs4)
        nc.sync.dma_start(out=counts[:], in_=old)
        nc.vector.memset(placed[:], 0.0)

        codes_b = sb.tile([P, Q], U32, name="codes_b", align_bytes=64)
        codes_a = sb.tile([P, Q], U32, name="codes_a", align_bytes=64)
        scales_b = sb.tile([P, Q], U8, name="scales_b", align_bytes=64)
        scales_a = sb.tile([P, Q], U8, name="scales_a", align_bytes=64)

        for raw, codes, scales in ((raw_b, codes_b, scales_b), (raw_a, codes_a, scales_a)):
            grouped = sb.tile([P, Q, PACK], BF16, name="grouped", align_bytes=64)
            rows = raw[:].rearrange("p j q -> p q j")
            nc.vector.tensor_copy(out=grouped[:, :CAST_SPLIT, :], in_=rows[:, :CAST_SPLIT, :])
            nc.scalar.activation(out=grouped[:, CAST_SPLIT:, :], in_=rows[:, CAST_SPLIT:, :], func=ACT.Copy)
            nc.vector.quantize_mx(
                out=codes[:].bitcast(FP8X4), scales=scales[:], in_=grouped[:].rearrange("p q j -> p (q j)")
            )

        a = sb.tile([P, T], F32, name="a")
        b = sb.tile([P, T], F32, name="b")

        def score(codes, scales, bank_name, t0, t1):
            bank = ps.tile([P, t1 - t0], F32, name=bank_name)
            load, first = divmod(t0, KEY_TOKENS)
            nc.tensor.matmul_mx(
                out=bank[:],
                lhsT=codes[:].bitcast(FP8X4),
                lhsT_scale=scales[:],
                rhs=key_words[load][:, WORD_BYTES * first : WORD_BYTES * (first + t1 - t0)].bitcast(FP4X4),
                rhs_scale=key_scales[:, t0:t1],
                start=True,
                stop=True,
            )
            return bank

        for n, (t0, t1) in enumerate(B_PIECES):
            bank = score(codes_b, scales_b, "bank_b%d" % n, t0, t1)
            if n % 2 == 0:
                nc.scalar.activation(out=b[:, t0:t1], in_=bank[:], func=ACT.Copy)
            else:
                nc.vector.tensor_copy(out=b[:, t0:t1], in_=bank[:])
        banks_a = [score(codes_a, scales_a, name, t0, t1) for name, (t0, t1) in zip(A_BANKS, A_PIECES)]
        a_cols = [slice(t0, t1) for t0, t1 in A_PIECES]
        for n in range(2):
            nc.vector.tensor_copy(out=a[:, a_cols[n]], in_=banks_a[n][:])

        neg_bar = sb.tile([P, 1], F32, name="neg_bar")
        nc.gpsimd.tensor_scalar(neg_bar[:], bar_col[:], -1.0 / RUN, 0.0, ALU.mult, ALU.add)

        def half_tiles(name):
            return [sb.tile([P, HALF], F32, name="%s%d" % (name, h)) for h in range(2)]

        tanh_b, a2_tanh_b, exp_s = (half_tiles(name) for name in ("tanh_b", "a2_tanh_b", "exp_s"))
        s = sb.tile([P, SLOTS], F32, name="s", tag="s_then_diff")
        halves = [slice(h * HALF, (h + 1) * HALF) for h in range(2)]
        b_picked = sb.tile([P, SLOTS], F32, name="b_picked")
        run_sum = [sb.tile([P, HALF // RUN], F32, name="run_sum%d" % h) for h in range(2)]
        r = sb.tile([P, SLOTS], F32, name="r")
        list_cols = [slice(h * HALF // LIST_ROWS, (h + 1) * HALF // LIST_ROWS) for h in range(2)]

        nc.scalar.activation(out=b_picked[:, halves[0]], in_=b[:].indirect(idx[:, list_cols[0]]), func=ACT.Copy)
        nc.vector.tensor_copy(out=b_picked[:, halves[1]], in_=b[:].indirect(idx[:, list_cols[1]]))
        nc.scalar.activation(out=a[:, a_cols[2]], in_=banks_a[2][:], func=ACT.Copy)
        nc.vector.tensor_copy(out=a[:, a_cols[3]], in_=banks_a[3][:])
        for h in range(2):
            nc.scalar.activation(out=tanh_b[h][:], in_=b_picked[:, halves[h]], func=ACT.Tanh)

        a_picked = sb.tile([P, SLOTS], F32, name="a_picked")
        for h in range(2):
            nc.scalar.activation(out=a_picked[:, halves[h]], in_=a[:].indirect(idx[:, list_cols[h]]), func=ACT.Copy)
        for h in range(2):
            nc.vector.tensor_tensor(a2_tanh_b[h][:], a[:].indirect(idx2[:, list_cols[h]]), tanh_b[h][:], ALU.mult)
        for h in range(2):
            nc.vector.scalar_tensor_tensor(
                s[:, halves[h]], a2_tanh_b[h][:], lam_col[:], a_picked[:, halves[h]], ALU.mult, ALU.add
            )
            nc.scalar.activation(out=exp_s[h][:], in_=s[:, halves[h]], func=ACT.Exp)

        runs = [exp_s[h][:].rearrange("q (g e) -> q g e", e=RUN) for h in range(2)]
        for h in range(2):
            nc.vector.tensor_reduce(run_sum[h][:], runs[h], AXIS.X, ALU.add)
        diff = sb.tile([P, SLOTS], F32, name="diff", tag="s_then_diff")
        for h in range(2):
            nc.vector.scalar_tensor_tensor(
                diff[:, halves[h]].rearrange("q (g e) -> q g e", e=RUN),
                run_sum[h][:].unsqueeze(2).to_broadcast([P, HALF // RUN, RUN]),
                neg_bar[:],
                runs[h],
                ALU.mult,
                ALU.add,
            )

        denom = sb.tile([P, 1], F32, name="denom")
        inv = sb.tile([P, 1], F32, name="inv")
        half_sum = sb.tile([P, 2], F32, name="half_sum")
        for h in range(2):
            nc.scalar.activation(
                out=r[:, halves[h]], in_=diff[:, halves[h]], func=ACT.Relu, accum_out=half_sum[:, h : h + 1]
            )
        nc.vector.tensor_scalar(denom[:], half_sum[:, 1:2], half_sum[:, 0:1], reserve_col[:], ALU.add, ALU.add)
        nc.vector.reciprocal(inv[:], denom[:])

        w256 = sb.tile([P, SLOTS], F32, name="w256")
        nc.vector.tensor_scalar(w256[:], r[:], inv[:], 256.0, ALU.mult, ALU.mult)
        nc.vector.tensor_tensor(placed[:].indirect(idx4[:]), w256[:], gain[:], ALU.mult)

        for n, (t0, t1) in enumerate(STORE_PIECES):
            piece = slice(t0, t1)
            result = sb.tile([P, t1 - t0], F32, name="result%d" % n)
            nc.vector.tensor_tensor(result[:], placed[:, piece], counts[:, piece], ALU.add)
            queue = nc.sync if n % 2 == 0 else nc.scalar
            queue.dma_start(out=out[:, piece], in_=result[:])
